import numpy as np
CORES = [36,164,52,180,100,228,116,244]
N = 8
TK = 128
D = 128 * N
EPS = 0.01
def setup_inputs(rng):
    return {"x": (rng.standard_normal((N, 128, TK), dtype=np.float32) * (0.5 + np.abs(rng.standard_normal((1, 1, TK), dtype=np.float32))) + rng.standard_normal((1, 1, TK), dtype=np.float32)), "w": (rng.standard_normal((N, 128, 128), dtype=np.float32) / 11)}
def reference(x, w):
    X = x.astype(np.float64)
    mu = X.sum(axis=(0, 1)) / D
    Z = X - mu
    Z = Z / np.sqrt((Z ** 2).sum(axis=(0, 1)) / D + EPS)
    s = sum(w[r].astype(np.float64).T @ Z[r] for r in range(N)).astype(np.float32)
    return {"y": np.broadcast_to(s, (N,) + s.shape)}

@@ -1,0 +1,151 @@
+from concourse.bass import DstId, RemoteDMATransfer
+from concourse.mybir import AluOpType, AxisListType, ActivationFunctionType
+
+N = 8
+D = 128 * N
+EPS = 0.01
+RADIX = (2, 4)
+PW = 131
+SLOT = 132
+
+SCRATCH = {
+    "xa": ("sbuf", [128, 132], "float32"),
+    "ws": ("sbuf", [128, 128], "float32"),
+    "xsq": ("sbuf", [128, 128], "float32"),
+    "ones": ("sbuf", [128, 128], "float32"),
+    "idd": ("sbuf", [128, 128], "float32"),
+    "dg": ("sbuf", [128, 128], "float32"),
+    "dmu": ("sbuf", [128, 128], "float32"),
+    "asum": ("sbuf", [128, 128], "float32"),
+    "tt": ("sbuf", [128, 128], "float32"),
+    "ysb": ("sbuf", [128, 128], "float32"),
+    "sc": ("sbuf", [128, 32], "float32"),
+    "ps": ("psum", [128, 512], "float32"),
+    "pmu": ("psum", [128, 512], "float32"),
+    "prs": ("psum", [128, 512], "float32"),
+}
+for _s, _r in enumerate(RADIX):
+    SCRATCH["b%d" % _s] = ("sbuf", [128, _r * SLOT], "float32")
+
+SEMAPHORES = ["lx", "lw", "loc", "st"] + ["a%d" % _s for _s in range(len(RADIX))] + ["k%d" % _i for _i in range(40)]
+
+
+def rank_program(g, core, T, topo):
+    rank = T.rank_of(core)
+    if rank is None:
+        return
+    V, ACT, PE, SY = g.vector, g.scalar, g.tensor, g.sync
+    add, mult = AluOpType.add, AluOpType.mult
+    nk = [0]
+
+    def new():
+        nk[0] += 1
+        return T.sem["k%d" % (nk[0] - 1)]
+
+    xa, ws, xsq, ones, idd, sc = T.xa, T.ws, T.xsq, T.ones, T.idd, T.sc
+    ps, pmu, prs = T.ps, T.pmu, T.prs
+
+    SY.dma_start(xa[:, 0:128], T.x[:]).then_inc(T.sem.lx, 16)
+    ACT.dma_start(ws[:], T.w[:]).then_inc(T.sem.lw, 16)
+    k_oc, k_dm, k_on, k_id = new(), new(), new(), new()
+    V.memset(xa[:, 128:132], 1.0).then_inc(k_oc, 1)
+    V.memset(idd[:], float(D)).then_inc(k_dm, 1)
+    V.memset(ones[:], 1.0).then_inc(k_on, 1)
+    g.wait_ge(k_dm, 1)
+    g.affine_select(idd[:], idd[:], [[-1, 128]], AluOpType.is_equal, 0.0, 0, 1).then_inc(k_id, 1)
+
+    k_sq, k_pe = new(), new()
+    ACT.wait_ge(T.sem.lx, 16)
+    ACT.activation(xsq[:], xa[:, 0:128], ActivationFunctionType.Square).then_inc(k_sq, 1)
+    PE.wait_ge(T.sem.lx, 16)
+    PE.wait_ge(k_oc, 1)
+    PE.matmul(ps[:, 129:130], xa[:, 0:128], xa[:, 128:129], True, True).then_inc(k_pe, 1)
+    PE.wait_ge(T.sem.lw, 16)
+    PE.matmul(ps[:, 0:129], ws[:], xa[:, 0:129], True, True).then_inc(k_pe, 1)
+    PE.wait_ge(k_sq, 1)
+    PE.matmul(ps[:, 130:131], xsq[:], xa[:, 128:129], True, True).then_inc(k_pe, 1)
+
+    k_own = new()
+    V.wait_ge(k_pe, 3)
+    V.tensor_copy(T.b0[:, 0:PW], ps[:, 0:PW]).then_inc(k_own, 1)
+
+    sent = 0
+    base = 1
+    for s, R in enumerate(RADIX):
+        b = T["b%d" % s]
+        dig = (rank // base) % R
+        ids, dsts, mask = [], [], -1
+        for k in range(1, R):
+            peer = T.cores[rank + (((dig + k) % R) - dig) * base]
+            rid, pid = topo.addr(peer, core)
+            ids.append(DstId(rid=rid, pnc=pid))
+            dsts.append(b[:, (R - k) * SLOT:(R - k) * SLOT + PW])
+            mask &= topo.mask(core, peer)
+        ne = bin(mask).count("1")
+        g.wait_ge(k_own, 1)
+        g.remote_dma_fused([RemoteDMATransfer(dst_ids=ids, dma_engine_mask=mask, remote_sem=T.sem["a%d" % s],
+                                              srcs=[b[:, 0:PW]], dsts=dsts)], local_sem=T.sem.loc)
+        sent += ne
+        V.wait_ge(T.sem["a%d" % s], ne * (R - 1))
+        if s == len(RADIX) - 1:
+            break
+        out = T["b%d" % (s + 1)][:, 0:PW]
+        acc = ps[:, 0:PW] if s == 0 else b[:, 0:PW]
+        if s > 0:
+            V.wait_ge(k_own, 1)
+        for k in range(1, R):
+            k_own = new()
+            V.tensor_tensor(out, acc, b[:, k * SLOT:k * SLOT + PW], add).then_inc(k_own, 1)
+            if k < R - 1:
+                V.wait_ge(k_own, 1)
+            acc = out
+        base *= R
+
+    V.wait_ge(k_own, 1)
+
+    def col(j):
+        return b[:, j:(R - 1) * SLOT + j + 1:SLOT]
+
+    S1, S2, tq, u, r, nm, C = [sc[:, 4 * i:4 * i + 1] for i in range(7)]
+    k1, k2, k3, k4, k5, k6, k7, k8, k9, k10 = [new() for _ in range(10)]
+    V.tensor_reduce(S1, col(129), AxisListType.X, add).then_inc(k1, 1)
+    V.tensor_reduce(S2, col(130), AxisListType.X, add).then_inc(k2, 1)
+    V.wait_ge(k1, 1)
+    V.tensor_scalar(tq, S1, S1, -1.0 / D, mult, mult).then_inc(k3, 1)
+    V.wait_ge(k2, 1)
+    V.wait_ge(k3, 1)
+    V.tensor_scalar(u, S2, tq, D * EPS, add, add).then_inc(k4, 1)
+    V.wait_ge(k4, 1)
+    V.reciprocal(r, u).then_inc(k5, 1)
+    ACT.wait_ge(k5, 1)
+    ACT.wait_ge(k_id, 1)
+    ACT.activation(T.dg[:], idd[:], ActivationFunctionType.Sqrt, scale=r).then_inc(k6, 1)
+    V.tensor_scalar(nm, S1, -1.0 / (D * D), None, mult).then_inc(k7, 1)
+    V.wait_ge(k7, 1)
+    V.wait_ge(k_id, 1)
+    V.tensor_scalar(T.dmu[:], idd[:], nm, None, mult).then_inc(k8, 1)
+    PE.wait_ge(k8, 1)
+    PE.wait_ge(k_on, 1)
+    PE.matmul(pmu[:, 0:128], ones[:], T.dmu[:], True, True).then_inc(k9, 1)
+    V.tensor_reduce(C, col(128), AxisListType.X, add).then_inc(k10, 1)
+    acc = b[:, 0:128]
+    for k in range(1, R):
+        k_sum = new()
+        V.tensor_tensor(T.asum[:], acc, b[:, k * SLOT:k * SLOT + 128], add).then_inc(k_sum, 1)
+        V.wait_ge(k_sum, 1)
+        acc = T.asum[:]
+    k11, k12, k13, k14 = [new() for _ in range(4)]
+    V.wait_ge(k9, 1)
+    V.wait_ge(k10, 1)
+    V.tensor_scalar(T.tt[:], pmu[:, 0:128], C, None, mult).then_inc(k11, 1)
+    V.wait_ge(k11, 1)
+    V.tensor_tensor(T.tt[:], T.tt[:], T.asum[:], add).then_inc(k12, 1)
+    PE.wait_ge(k6, 1)
+    PE.matmul(prs[:, 0:128], ones[:], T.dg[:], True, True).then_inc(k13, 1)
+    V.wait_ge(k12, 1)
+    V.wait_ge(k13, 1)
+    V.tensor_tensor(T.ysb[:], T.tt[:], prs[:, 0:128], mult).then_inc(k14, 1)
+    SY.wait_ge(k14, 1)
+    SY.dma_start(T.y[:], T.ysb[:]).then_inc(T.sem.st, 16)
+    SY.wait_ge(T.sem.st, 16)
+    g.wait_ge(T.sem.loc, sent)

@@ -5,8 +5,10 @@ N = 8
 D = 128 * N
 EPS = 0.01
 RADIX = (2, 4)
-PW = 131
-SLOT = 132
+PW = 128
+P0 = 132
+SW = 4
+NFAR = N - RADIX[0]
 
 SCRATCH = {
     "xa": ("sbuf", [128, 132], "float32"),
@@ -16,18 +18,19 @@ SCRATCH = {
     "idd": ("sbuf", [128, 128], "float32"),
     "dg": ("sbuf", [128, 128], "float32"),
     "dmu": ("sbuf", [128, 128], "float32"),
-    "asum": ("sbuf", [128, 128], "float32"),
     "tt": ("sbuf", [128, 128], "float32"),
     "ysb": ("sbuf", [128, 128], "float32"),
+    "sb": ("sbuf", [128, (NFAR + 1) * SW], "float32"),
     "sc": ("sbuf", [128, 32], "float32"),
+    "b0": ("sbuf", [128, RADIX[0] * P0], "float32"),
+    "b1": ("sbuf", [128, RADIX[1] * PW], "float32"),
     "ps": ("psum", [128, 512], "float32"),
+    "pst": ("psum", [128, 512], "float32"),
     "pmu": ("psum", [128, 512], "float32"),
     "prs": ("psum", [128, 512], "float32"),
 }
-for _s, _r in enumerate(RADIX):
-    SCRATCH["b%d" % _s] = ("sbuf", [128, _r * SLOT], "float32")
 
-SEMAPHORES = ["lx", "lw", "loc", "st"] + ["a%d" % _s for _s in range(len(RADIX))] + ["k%d" % _i for _i in range(40)]
+SEMAPHORES = ["lx", "lw", "loc", "st", "astat", "a0", "a1"] + ["k%d" % _i for _i in range(40)]
 
 
 def rank_program(g, core, T, topo):
@@ -36,14 +39,30 @@ def rank_program(g, core, T, topo):
         return
     V, ACT, PE, SY = g.vector, g.scalar, g.tensor, g.sync
     add, mult = AluOpType.add, AluOpType.mult
+    R0, R1 = RADIX
     nk = [0]
 
     def new():
         nk[0] += 1
         return T.sem["k%d" % (nk[0] - 1)]
 
-    xa, ws, xsq, ones, idd, sc = T.xa, T.ws, T.xsq, T.ones, T.idd, T.sc
-    ps, pmu, prs = T.ps, T.pmu, T.prs
+    def send(src, ranks, dsts, sem):
+        ids, mask = [], -1
+        for q in ranks:
+            rid, pid = topo.addr(T.cores[q], core)
+            ids.append(DstId(rid=rid, pnc=pid))
+            mask &= topo.mask(core, T.cores[q])
+        g.remote_dma_fused([RemoteDMATransfer(dst_ids=ids, dma_engine_mask=mask, remote_sem=sem, srcs=[src], dsts=dsts)],
+                           local_sem=T.sem.loc)
+        return bin(mask).count("1")
+
+    def far(q):
+        return [p for p in range(N) if p // R0 != q // R0]
+
+    xa, ws, xsq, ones, idd, sc, sb, b0, b1 = T.xa, T.ws, T.xsq, T.ones, T.idd, T.sc, T.sb, T.b0, T.b1
+    ps, pst, prs = T.ps, T.pst, T.prs
+    pm = T.pmu[:, 0:128]
+    one = xa[:, 128:129]
 
     SY.dma_start(xa[:, 0:128], T.x[:]).then_inc(T.sem.lx, 16)
     ACT.dma_start(ws[:], T.w[:]).then_inc(T.sem.lw, 16)
@@ -54,62 +73,60 @@ def rank_program(g, core, T, topo):
     g.wait_ge(k_dm, 1)
     g.affine_select(idd[:], idd[:], [[-1, 128]], AluOpType.is_equal, 0.0, 0, 1).then_inc(k_id, 1)
 
-    k_sq, k_pe = new(), new()
+    k_sq, k_a, k_pe, k_own = new(), new(), new(), new()
     ACT.wait_ge(T.sem.lx, 16)
     ACT.activation(xsq[:], xa[:, 0:128], ActivationFunctionType.Square).then_inc(k_sq, 1)
     PE.wait_ge(T.sem.lx, 16)
     PE.wait_ge(k_oc, 1)
-    PE.matmul(ps[:, 129:130], xa[:, 0:128], xa[:, 128:129], True, True).then_inc(k_pe, 1)
+    PE.matmul(pst[:, 0:1], xa[:, 0:128], one, True, True).then_inc(k_pe, 1)
     PE.wait_ge(T.sem.lw, 16)
-    PE.matmul(ps[:, 0:129], ws[:], xa[:, 0:129], True, True).then_inc(k_pe, 1)
+    PE.matmul(ps[:, 0:129], ws[:], xa[:, 0:129], True, True).then_inc(k_a, 1)
     PE.wait_ge(k_sq, 1)
-    PE.matmul(ps[:, 130:131], xsq[:], xa[:, 128:129], True, True).then_inc(k_pe, 1)
+    PE.matmul(pst[:, 1:2], xsq[:], one, True, True).then_inc(k_pe, 1)
+    V.wait_ge(k_a, 1)
+    V.tensor_copy(b0[:, 0:129], ps[:, 0:129]).then_inc(k_own, 1)
+    V.wait_ge(k_pe, 2)
+    V.tensor_copy(b0[:, 129:131], pst[:, 0:2]).then_inc(k_own, 1)
 
-    k_own = new()
-    V.wait_ge(k_pe, 3)
-    V.tensor_copy(T.b0[:, 0:PW], ps[:, 0:PW]).then_inc(k_own, 1)
+    d0 = rank % R0
+    g.wait_ge(k_own, 2)
+    n0 = send(b0[:, 0:131], [rank - d0 + (d0 + k) % R0 for k in range(1, R0)],
+              [b0[:, (R0 - k) * P0:(R0 - k) * P0 + 131] for k in range(1, R0)], T.sem.a0)
+    nst = send(b0[:, 128:131], far(rank),
+               [sb[:, (1 + far(q).index(rank)) * SW:(1 + far(q).index(rank)) * SW + 3] for q in far(rank)], T.sem.astat)
 
-    sent = 0
-    base = 1
-    for s, R in enumerate(RADIX):
-        b = T["b%d" % s]
-        dig = (rank // base) % R
-        ids, dsts, mask = [], [], -1
-        for k in range(1, R):
-            peer = T.cores[rank + (((dig + k) % R) - dig) * base]
-            rid, pid = topo.addr(peer, core)
-            ids.append(DstId(rid=rid, pnc=pid))
-            dsts.append(b[:, (R - k) * SLOT:(R - k) * SLOT + PW])
-            mask &= topo.mask(core, peer)
-        ne = bin(mask).count("1")
-        g.wait_ge(k_own, 1)
-        g.remote_dma_fused([RemoteDMATransfer(dst_ids=ids, dma_engine_mask=mask, remote_sem=T.sem["a%d" % s],
-                                              srcs=[b[:, 0:PW]], dsts=dsts)], local_sem=T.sem.loc)
-        sent += ne
-        V.wait_ge(T.sem["a%d" % s], ne * (R - 1))
-        if s == len(RADIX) - 1:
-            break
-        out = T["b%d" % (s + 1)][:, 0:PW]
-        acc = ps[:, 0:PW] if s == 0 else b[:, 0:PW]
-        if s > 0:
-            V.wait_ge(k_own, 1)
-        for k in range(1, R):
-            k_own = new()
-            V.tensor_tensor(out, acc, b[:, k * SLOT:k * SLOT + PW], add).then_inc(k_own, 1)
-            if k < R - 1:
-                V.wait_ge(k_own, 1)
-            acc = out
-        base *= R
+    k_p = None
+    V.wait_ge(T.sem.a0, n0 * (R0 - 1))
+    for k in range(1, R0):
+        if k_p is not None:
+            V.wait_ge(k_p, 1)
+        k_p = new()
+        V.tensor_tensor(ps[:, 0:PW] if k < R0 - 1 else b1[:, 0:PW], ps[:, 0:PW], b0[:, k * P0:k * P0 + PW],
+                        add).then_inc(k_p, 1)
 
-    V.wait_ge(k_own, 1)
+    d1 = rank // R0
+    g.wait_ge(k_p, 1)
+    n1 = send(b1[:, 0:PW], [((d1 + k) % R1) * R0 + d0 for k in range(1, R1)],
+              [b1[:, (R1 - k) * PW:(R1 - k + 1) * PW] for k in range(1, R1)], T.sem.a1)
+
+    k_g = None
+    V.wait_ge(k_own, 2)
+    for k in range(1, R0):
+        if k_g is not None:
+            V.wait_ge(k_g, 1)
+        k_g = new()
+        V.tensor_tensor(sb[:, 0:3], b0[:, 128:131] if k == 1 else sb[:, 0:3], b0[:, k * P0 + 128:k * P0 + 131],
+                        add).then_inc(k_g, 1)
 
     def col(j):
-        return b[:, j:(R - 1) * SLOT + j + 1:SLOT]
+        return sb[:, j:NFAR * SW + j + 1:SW]
 
     S1, S2, tq, u, r, nm, C = [sc[:, 4 * i:4 * i + 1] for i in range(7)]
-    k1, k2, k3, k4, k5, k6, k7, k8, k9, k10 = [new() for _ in range(10)]
-    V.tensor_reduce(S1, col(129), AxisListType.X, add).then_inc(k1, 1)
-    V.tensor_reduce(S2, col(130), AxisListType.X, add).then_inc(k2, 1)
+    k1, k2, k3, k4, k5, k6, k7, k8, k9, k10, k11, k12, k13, k14 = [new() for _ in range(14)]
+    V.wait_ge(T.sem.astat, nst * NFAR)
+    V.wait_ge(k_g, 1)
+    V.tensor_reduce(S1, col(1), AxisListType.X, add).then_inc(k1, 1)
+    V.tensor_reduce(S2, col(2), AxisListType.X, add).then_inc(k2, 1)
     V.wait_ge(k1, 1)
     V.tensor_scalar(tq, S1, S1, -1.0 / D, mult, mult).then_inc(k3, 1)
     V.wait_ge(k2, 1)
@@ -126,26 +143,27 @@ def rank_program(g, core, T, topo):
     V.tensor_scalar(T.dmu[:], idd[:], nm, None, mult).then_inc(k8, 1)
     PE.wait_ge(k8, 1)
     PE.wait_ge(k_on, 1)
-    PE.matmul(pmu[:, 0:128], ones[:], T.dmu[:], True, True).then_inc(k9, 1)
-    V.tensor_reduce(C, col(128), AxisListType.X, add).then_inc(k10, 1)
-    acc = b[:, 0:128]
-    for k in range(1, R):
-        k_sum = new()
-        V.tensor_tensor(T.asum[:], acc, b[:, k * SLOT:k * SLOT + 128], add).then_inc(k_sum, 1)
-        V.wait_ge(k_sum, 1)
-        acc = T.asum[:]
-    k11, k12, k13, k14 = [new() for _ in range(4)]
-    V.wait_ge(k9, 1)
-    V.wait_ge(k10, 1)
-    V.tensor_scalar(T.tt[:], pmu[:, 0:128], C, None, mult).then_inc(k11, 1)
-    V.wait_ge(k11, 1)
-    V.tensor_tensor(T.tt[:], T.tt[:], T.asum[:], add).then_inc(k12, 1)
+    PE.matmul(pm, ones[:], T.dmu[:], True, True).then_inc(k9, 1)
     PE.wait_ge(k6, 1)
     PE.matmul(prs[:, 0:128], ones[:], T.dg[:], True, True).then_inc(k13, 1)
-    V.wait_ge(k12, 1)
+    V.tensor_reduce(C, col(0), AxisListType.X, add).then_inc(k10, 1)
+    V.wait_ge(k9, 1)
+    V.wait_ge(k10, 1)
+    V.tensor_scalar(pm, pm, C, None, mult).then_inc(k11, 1)
+    V.wait_ge(k11, 1)
+    V.wait_ge(k_p, 1)
+    V.tensor_tensor(pm, pm, b1[:, 0:PW], add).then_inc(k12, 1)
+
+    V.wait_ge(T.sem.a1, n1 * (R1 - 1))
+    k_prev = k12
+    for k in range(1, R1):
+        V.wait_ge(k_prev, 1)
+        k_prev = new()
+        V.tensor_tensor(pm if k < R1 - 1 else T.tt[:], pm, b1[:, k * PW:(k + 1) * PW], add).then_inc(k_prev, 1)
+    V.wait_ge(k_prev, 1)
     V.wait_ge(k13, 1)
     V.tensor_tensor(T.ysb[:], T.tt[:], prs[:, 0:128], mult).then_inc(k14, 1)
     SY.wait_ge(k14, 1)
     SY.dma_start(T.y[:], T.ysb[:]).then_inc(T.sem.st, 16)
     SY.wait_ge(T.sem.st, 16)
-    g.wait_ge(T.sem.loc, sent)
+    g.wait_ge(T.sem.loc, n0 + nst + n1)

from concourse.bass import DstId, RemoteDMATransfer
from concourse.mybir import AluOpType, AxisListType, ActivationFunctionType

N = 8
D = 128 * N
EPS = 0.01
RADIX = (2, 4)
PW = 128
P0 = 132
SW = 4
NFAR = N - RADIX[0]

SCRATCH = {
    "xa": ("sbuf", [128, 132], "float32"),
    "ws": ("sbuf", [128, 128], "float32"),
    "xsq": ("sbuf", [128, 128], "float32"),
    "ones": ("sbuf", [128, 128], "float32"),
    "idd": ("sbuf", [128, 128], "float32"),
    "dg": ("sbuf", [128, 128], "float32"),
    "dmu": ("sbuf", [128, 128], "float32"),
    "tt": ("sbuf", [128, 128], "float32"),
    "ysb": ("sbuf", [128, 128], "float32"),
    "sb": ("sbuf", [128, (NFAR + 1) * SW], "float32"),
    "sc": ("sbuf", [128, 32], "float32"),
    "b0": ("sbuf", [128, RADIX[0] * P0], "float32"),
    "b1": ("sbuf", [128, RADIX[1] * PW], "float32"),
    "ps": ("psum", [128, 512], "float32"),
    "pst": ("psum", [128, 512], "float32"),
    "pmu": ("psum", [128, 512], "float32"),
    "prs": ("psum", [128, 512], "float32"),
}

SEMAPHORES = ["lx", "lw", "loc", "st", "astat", "a0", "a1"] + ["k%d" % _i for _i in range(40)]


def rank_program(g, core, T, topo):
    rank = T.rank_of(core)
    if rank is None:
        return
    V, ACT, PE, SY = g.vector, g.scalar, g.tensor, g.sync
    add, mult = AluOpType.add, AluOpType.mult
    R0, R1 = RADIX
    nk = [0]

    def new():
        nk[0] += 1
        return T.sem["k%d" % (nk[0] - 1)]

    def send(src, ranks, dsts, sem):
        ids, mask = [], -1
        for q in ranks:
            rid, pid = topo.addr(T.cores[q], core)
            ids.append(DstId(rid=rid, pnc=pid))
            mask &= topo.mask(core, T.cores[q])
        g.remote_dma_fused([RemoteDMATransfer(dst_ids=ids, dma_engine_mask=mask, remote_sem=sem, srcs=[src], dsts=dsts)],
                           local_sem=T.sem.loc)
        return bin(mask).count("1")

    def far(q):
        return [p for p in range(N) if p // R0 != q // R0]

    xa, ws, xsq, ones, idd, sc, sb, b0, b1 = T.xa, T.ws, T.xsq, T.ones, T.idd, T.sc, T.sb, T.b0, T.b1
    ps, pst, prs = T.ps, T.pst, T.prs
    pm = T.pmu[:, 0:128]
    one = xa[:, 128:129]

    SY.dma_start(xa[:, 0:128], T.x[:]).then_inc(T.sem.lx, 16)
    ACT.dma_start(ws[:], T.w[:]).then_inc(T.sem.lw, 16)
    k_oc, k_dm, k_on, k_id = new(), new(), new(), new()
    V.memset(xa[:, 128:132], 1.0).then_inc(k_oc, 1)
    V.memset(idd[:], float(D)).then_inc(k_dm, 1)
    V.memset(ones[:], 1.0).then_inc(k_on, 1)
    g.wait_ge(k_dm, 1)
    g.affine_select(idd[:], idd[:], [[-1, 128]], AluOpType.is_equal, 0.0, 0, 1).then_inc(k_id, 1)

    k_sq, k_a, k_pe, k_own = new(), new(), new(), new()
    ACT.wait_ge(T.sem.lx, 16)
    ACT.activation(xsq[:], xa[:, 0:128], ActivationFunctionType.Square).then_inc(k_sq, 1)
    PE.wait_ge(T.sem.lx, 16)
    PE.wait_ge(k_oc, 1)
    PE.matmul(pst[:, 0:1], xa[:, 0:128], one, True, True).then_inc(k_pe, 1)
    PE.wait_ge(T.sem.lw, 16)
    PE.matmul(ps[:, 0:129], ws[:], xa[:, 0:129], True, True).then_inc(k_a, 1)
    PE.wait_ge(k_sq, 1)
    PE.matmul(pst[:, 1:2], xsq[:], one, True, True).then_inc(k_pe, 1)
    V.wait_ge(k_a, 1)
    V.tensor_copy(b0[:, 0:129], ps[:, 0:129]).then_inc(k_own, 1)
    V.wait_ge(k_pe, 2)
    V.tensor_copy(b0[:, 129:131], pst[:, 0:2]).then_inc(k_own, 1)

    d0 = rank % R0
    g.wait_ge(k_own, 2)
    n0 = send(b0[:, 0:131], [rank - d0 + (d0 + k) % R0 for k in range(1, R0)],
              [b0[:, (R0 - k) * P0:(R0 - k) * P0 + 131] for k in range(1, R0)], T.sem.a0)
    nst = send(b0[:, 128:131], far(rank),
               [sb[:, (1 + far(q).index(rank)) * SW:(1 + far(q).index(rank)) * SW + 3] for q in far(rank)], T.sem.astat)

    k_p = None
    V.wait_ge(T.sem.a0, n0 * (R0 - 1))
    for k in range(1, R0):
        if k_p is not None:
            V.wait_ge(k_p, 1)
        k_p = new()
        V.tensor_tensor(ps[:, 0:PW] if k < R0 - 1 else b1[:, 0:PW], ps[:, 0:PW], b0[:, k * P0:k * P0 + PW],
                        add).then_inc(k_p, 1)

    d1 = rank // R0
    g.wait_ge(k_p, 1)
    n1 = send(b1[:, 0:PW], [((d1 + k) % R1) * R0 + d0 for k in range(1, R1)],
              [b1[:, (R1 - k) * PW:(R1 - k + 1) * PW] for k in range(1, R1)], T.sem.a1)

    k_g = None
    V.wait_ge(k_own, 2)
    for k in range(1, R0):
        if k_g is not None:
            V.wait_ge(k_g, 1)
        k_g = new()
        V.tensor_tensor(sb[:, 0:3], b0[:, 128:131] if k == 1 else sb[:, 0:3], b0[:, k * P0 + 128:k * P0 + 131],
                        add).then_inc(k_g, 1)

    def col(j):
        return sb[:, j:NFAR * SW + j + 1:SW]

    S1, S2, tq, u, r, nm, C = [sc[:, 4 * i:4 * i + 1] for i in range(7)]
    k1, k2, k3, k4, k5, k6, k7, k8, k9, k10, k11, k12, k13, k14 = [new() for _ in range(14)]
    V.wait_ge(T.sem.astat, nst * NFAR)
    V.wait_ge(k_g, 1)
    V.tensor_reduce(S1, col(1), AxisListType.X, add).then_inc(k1, 1)
    V.tensor_reduce(S2, col(2), AxisListType.X, add).then_inc(k2, 1)
    V.wait_ge(k1, 1)
    V.tensor_scalar(tq, S1, S1, -1.0 / D, mult, mult).then_inc(k3, 1)
    V.wait_ge(k2, 1)
    V.wait_ge(k3, 1)
    V.tensor_scalar(u, S2, tq, D * EPS, add, add).then_inc(k4, 1)
    V.wait_ge(k4, 1)
    V.reciprocal(r, u).then_inc(k5, 1)
    ACT.wait_ge(k5, 1)
    ACT.wait_ge(k_id, 1)
    ACT.activation(T.dg[:], idd[:], ActivationFunctionType.Sqrt, scale=r).then_inc(k6, 1)
    V.tensor_scalar(nm, S1, -1.0 / (D * D), None, mult).then_inc(k7, 1)
    V.wait_ge(k7, 1)
    V.wait_ge(k_id, 1)
    V.tensor_scalar(T.dmu[:], idd[:], nm, None, mult).then_inc(k8, 1)
    PE.wait_ge(k8, 1)
    PE.wait_ge(k_on, 1)
    PE.matmul(pm, ones[:], T.dmu[:], True, True).then_inc(k9, 1)
    PE.wait_ge(k6, 1)
    PE.matmul(prs[:, 0:128], ones[:], T.dg[:], True, True).then_inc(k13, 1)
    V.tensor_reduce(C, col(0), AxisListType.X, add).then_inc(k10, 1)
    V.wait_ge(k9, 1)
    V.wait_ge(k10, 1)
    V.tensor_scalar(pm, pm, C, None, mult).then_inc(k11, 1)
    V.wait_ge(k11, 1)
    V.wait_ge(k_p, 1)
    V.tensor_tensor(pm, pm, b1[:, 0:PW], add).then_inc(k12, 1)

    V.wait_ge(T.sem.a1, n1 * (R1 - 1))
    k_prev = k12
    for k in range(1, R1):
        V.wait_ge(k_prev, 1)
        k_prev = new()
        V.tensor_tensor(pm if k < R1 - 1 else T.tt[:], pm, b1[:, k * PW:(k + 1) * PW], add).then_inc(k_prev, 1)
    V.wait_ge(k_prev, 1)
    V.wait_ge(k13, 1)
    V.tensor_tensor(T.ysb[:], T.tt[:], prs[:, 0:128], mult).then_inc(k14, 1)
    SY.wait_ge(k14, 1)
    SY.dma_start(T.y[:], T.ysb[:]).then_inc(T.sem.st, 16)
    SY.wait_ge(T.sem.st, 16)
    g.wait_ge(T.sem.loc, n0 + nst + n1)
